import numpy as np, ml_dtypes
CORES = [2,10,34,50,74,82,98,114,130,138,162,178,202,210,226,242]
N = 16
J, Q = 1024, 4096
def entries(a): return a.T.reshape(-1)
def pack(v, P): return np.ascontiguousarray(np.asarray(v, np.int32).reshape(-1, P).T)
def split(rng, total, parts):
    c = np.sort(rng.integers(0, total + 1, parts - 1)); return np.diff(np.concatenate([[0], c, [total]]))
def lists(rng, how):
    s = np.concatenate([[0], rng.integers(1 - Q // 2, Q // 2 + 1, N - 1), [int(rng.integers(1 - Q // 2, 1))]])
    if how == "early": s[1:] = -Q; s[N] = -2 * Q
    if how == "late": s[1:] = Q; s[N] = 0
    if how == "long":
        z = int(rng.integers(1, N - 1)); s[1:z] = -rng.integers(1, Q, z - 1); s[z] = -Q; s[z + 1] = Q; s[z + 2:N] = rng.integers(1, Q, N - z - 2); s[N] = -int(rng.integers(0, Q - s[N - 1] + 1))
    if how == "sway":
        z = int(rng.integers(1, N - 2)); e = int(rng.integers(z + 1, N - 1)); s[1:] = -rng.integers(Q // 2 + 1, Q, N); s[z + 1:e + 1] = rng.integers(Q // 2 + 1, Q - 1, e - z); s[e + 1] = s[e] - Q; s[N] = s[N - 1] - Q + int(rng.integers(1, -s[N - 1]))
    tot = Q + np.diff(s)
    L = np.stack([split(rng, int(t), J) for t in tot])
    if how == "gaps":
        L = np.zeros((N, J), np.int64)
        for r in range(N): m = 1 if r & 1 else 8; L[r, 1 + rng.permutation(J - 2)[:m]] = split(rng, int(tot[r]), m)
    if how == "long":
        L = np.zeros((N, J), np.int64); L[np.arange(N), rng.integers(0, J, N)] = tot
    return {"ln": np.stack([pack(l, 16) for l in L])}
def setup_inputs(rng):
    return dict({"x": rng.standard_normal((N, 128, J), dtype=np.float32).astype(ml_dtypes.bfloat16)}, **lists(rng, "uniform"))
def setup_inputs_early(rng):
    d = setup_inputs(rng); d.update(lists(rng, "early"))
    for k in ("x",): d[k] = (d[k].astype(np.float32) * 1048576.0).astype(d[k].dtype)
    return d
def setup_inputs_gaps(rng):
    d = setup_inputs(rng); d.update(lists(rng, "gaps"))
    for k in ("x",): d[k] = (d[k].astype(np.float32) * (1 / 1024.0)).astype(d[k].dtype)
    return d
def setup_inputs_late(rng):
    d = setup_inputs(rng); d.update(lists(rng, "late"))
    return d
def setup_inputs_long(rng):
    d = setup_inputs(rng); d.update(lists(rng, "long"))
    return d
def setup_inputs_sway(rng):
    d = setup_inputs(rng); d.update(lists(rng, "sway"))
    return d
def check_inputs(x):
    bad = []
    if x["ln"].min() < 0 or x["ln"].max() >= N * Q + 1: bad.append("ln out of range")
    if int(x["ln"].sum()) > N * Q: bad.append("the lengths come to more than N * Q")
    c = np.concatenate([[0], np.cumsum([int(a.sum()) for a in x["ln"]])])
    if any(c[r] < (r - 1) * Q or c[r + 1] > (r + 2) * Q for r in range(N)): bad.append("the sums of the lengths before or up to a rank leave their bounds")
    return bad
def reference(x, ln):
    got = np.concatenate([np.repeat(x[r], entries(ln[r]), axis=1) for r in range(N)], axis=1)[:, :N * Q]
    Y = np.zeros((128, N * Q), x.dtype); Y[:, :got.shape[1]] = got
    return {"y": np.stack([Y[:, Q * r:Q * r + Q] for r in range(N)])}

from concourse.bass import DstId, RemoteDMATransfer
from concourse.mybir import AluOpType as A, AxisListType, ActivationFunctionType as F

SCRATCH = {
    "lall": ("dram", [16, 128, 8], "int32"),
    "xw": ("sbuf", [128, 3088], "bfloat16"),
    "yb": ("sbuf", [128, 4096], "bfloat16"),
    "la": ("sbuf", [128, 128], "int32"),
    "pl": ("sbuf", [128, 64], "int32"),
    "lf": ("sbuf", [128, 128], "float32"),
    "cr": ("sbuf", [128, 128], "float32"),
    "s2": ("sbuf", [128, 64], "float32"),
    "tot": ("sbuf", [128, 4], "float32"),
    "rr": ("sbuf", [128, 24], "float32"),
    "ones": ("sbuf", [128, 128], "float32"),
    "jj": ("sbuf", [128, 512], "bfloat16"),
    "col": ("sbuf", [128, 16], "float32"),
    "ia": ("sbuf", [128, 66], "bfloat16"),
    "beta": ("sbuf", [128, 64], "bfloat16"),
    "m1": ("sbuf", [128, 24], "float32"),
    "m2": ("sbuf", [128, 24], "float32"),
    "m3": ("sbuf", [128, 24], "float32"),
    "selt": ("sbuf", [128, 24], "float32"),
    "selg": ("sbuf", [128, 24], "float32"),
    "sela": ("sbuf", [128, 24], "float32"),
    "eq": ("sbuf", [128, 512], "bfloat16"),
    "si": ("sbuf", [128, 512], "bfloat16"),
    "se": ("sbuf", [128, 512], "bfloat16"),
    "ai": ("sbuf", [128, 24], "int32"),
    "nf": ("sbuf", [128, 24], "float32"),
    "sta": ("sbuf", [128, 24 * 66], "bfloat16"),
    "stb": ("sbuf", [128, 24 * 64], "bfloat16"),
    "xy": ("sbuf", [128, 66], "bfloat16"),
    "off": ("sbuf", [128, 256], "uint16"),
    "ep": ("psum", [128, 512], "float32"),
    "yp": ("psum", [128, 512], "float32"),
    "cn": ("psum", [128, 512], "float32"),
}
SEMAPHORES = ["s_ln", "s_x", "ln_near", "ln_far", "x_arr", "h_arr", "snd_ln", "snd_x", "s_pl", "s_la",
              "sg", "sv", "sa", "sb", "sp", "gv", "gs", "sst"]

CH_S = [40, 40, 32, 16]
CH_V = [40, 40, 32, 16]


def _bits(m):
    return [1 << i for i in range(16) if (m >> i) & 1]


def _helpers(T, topo, r):
    me = T.cores[r]
    lo = me - me % topo.CORES_PER_CHIP
    near = [c for c in range(lo, lo + topo.CORES_PER_CHIP) if c != me]
    out = []
    for d, slot, same in ((r + 1, 0, True), (r - 1, 2, False)):
        if 0 <= d < len(T.cores):
            h = [c for c in near if topo.may_write(c, T.cores[d]) and (topo.die(c) == topo.die(me)) == same
                 and c not in [o[0] for o in out]][0]
            out.append((h, d, slot))
    return out


def rank_program(g, core, T, topo):
    n = len(T.cores)
    r = T.rank_of(core)
    S = T.sem
    if r is None:
        for q in range(n):
            for h, d, slot in _helpers(T, topo, q):
                if h == core:
                    dst = T.cores[d]
                    rid, pid = topo.addr(dst, core)
                    m = topo.mask(core, dst)
                    g.wait_ge(S.h_arr, len(_bits(topo.mask(T.cores[q], core))))
                    g.remote_dma(T.xw[:, 1024 * slot:1024 * slot + 1024], T.xw[:, 1024:2048], S.x_arr, S.snd_x,
                                 pid, rid, m)
                    g.wait_ge(S.snd_x, len(_bits(m)))
        return

    nb = [d for d in (r - 1, r + 1) if 0 <= d < n]
    far_src = max(r - 1, 0)
    kb = 8 * (r + 1)
    n_off = len(_bits(topo.mask(core, T.cores[nb[0]])))

    g.sync.dma_start(T.lall[r], T.ln[:]).then_inc(S.s_ln, 16)
    g.sync.dma_start(T.xw[:, 1024:2048], T.x[:]).then_inc(S.s_x, 16)

    g.iota(T.col[:, 0:1], [[0, 1]], 0, 1, allow_small_or_imprecise_dtypes=True).then_inc(S.sg, 1)
    g.iota(T.jj[:], [[16, 4], [0, 8], [1, 16]], 0, 0, allow_small_or_imprecise_dtypes=True).then_inc(S.sg, 1)
    g.wait_ge(S.s_ln, 16)
    eng = _bits(topo.mask(core, T.cores[nb[0]]))[::2]
    far = [d for d in range(r + 2, n)]
    groups = [(nb, S.ln_near)] + [(far[i::len(eng) - 1], S.ln_far) for i in range(len(eng) - 1)]
    tr = []
    for i, (ds, sem) in enumerate(groups):
        if ds:
            ids = []
            for d in ds:
                rid, pid = topo.addr(T.cores[d], core)
                ids.append(DstId(rid=rid, pnc=pid))
            tr.append(RemoteDMATransfer(dst_ids=ids, dma_engine_mask=eng[i], remote_sem=sem,
                                        srcs=[T.lall[r]], dsts=[T.lall[r] for d in ds]))
    g.remote_dma_fused(tr, local_sem=S.snd_ln)
    g.wait_ge(S.s_x, 16)
    hs = [h for h, d, slot in _helpers(T, topo, r)]
    ids = []
    for h in hs:
        rid, pid = topo.addr(h, core)
        ids.append(DstId(rid=rid, pnc=pid))
    hm = topo.mask(core, hs[0])
    g.remote_dma_fused([RemoteDMATransfer(dst_ids=ids, dma_engine_mask=hm, remote_sem=S.h_arr,
                                          srcs=[T.xw[:, 1024:2048]], dsts=[T.xw[:, 1024:2048] for h in hs])],
                       local_sem=S.snd_x)

    nv = [0]

    def v(ins):
        ins.then_inc(S.sv, 1)
        nv[0] += 1
        return nv[0]

    def vw():
        g.vector.wait_ge(S.sv, nv[0])

    ts = g.vector.tensor_scalar
    tt = g.vector.tensor_tensor
    p_, t_, cc, pc2, b_, h8, c63, pgt, b16 = [T.col[:, i:i + 1] for i in range(9)]
    edge = len(nb) < 2
    if edge:
        n_edge = v(g.vector.memset(T.pl[:], 0))
        s = 0 if r == 0 else 2
        v(g.vector.memset(T.xw[:, 1024 * s:1024 * s + 1024], 0.0))
    v(g.vector.memset(T.xw[:, 3072:3088], 0.0))
    v(g.vector.memset(T.ones[:], 1.0))
    v(g.vector.memset(T.lf[:], 0.0))
    v(g.vector.memset(T.ia[:, 64:66], 63.5))
    g.vector.wait_ge(S.sg, 2)
    v(ts(t_, p_, 64.0, -64.0, A.is_ge, A.mult))
    v(ts(cc, p_, 0.0, -(64.0 * r + 63.0 / 128.0), A.is_equal, A.mult))
    v(ts(pc2, p_, 2.0, -16.0 * (r - 1), A.mult, A.add))
    for u in range(4):
        v(ts(T.ia[:, 16 * u:16 * u + 16], T.jj[:, 128 * u:128 * u + 16], 0.5, None, A.subtract))
        v(ts(T.beta[:, 16 * u:16 * u + 16], T.jj[:, 128 * u:128 * u + 16], 1.0 / 64, 31.0 / 64, A.mult, A.subtract))
    vw()
    v(tt(b_, t_, p_, A.add))
    v(ts(h8, t_, -8.0 / 64, None, A.mult))
    vw()
    v(ts(c63, b_, 63.0, 0.5, A.is_equal, A.mult))
    v(tt(pgt, b_, h8, A.subtract))
    v(ts(b16, b_, 16.0, None, A.subtract))
    vw()
    for w in range(3):
        o = slice(8 * w, 8 * w + 8)
        j1 = T.jj[:, 128 * w:128 * w + 8]
        j0 = T.jj[:, 128 * w:128 * w + 128:16]
        v(ts(T.m1[:, o], j1, pgt, -1.0 / 64, A.is_lt, A.mult))
        v(ts(T.m2[:, o], j0, b16, None, A.is_gt))
        v(ts(T.m3[:, o], j0, b_, 1.0 / 64, A.is_le, A.mult))
        v(ts(T.selt[:, o], j0, pc2, 1.0 / 64, A.is_gt, A.mult))
    v(ts(T.eq[:], T.jj[:], b_, 0.5, A.is_equal, A.mult))
    vw()
    v(tt(T.selg[:], T.m1[:], T.m2[:], A.mult))
    v(tt(T.sela[:], T.m3[:], T.m2[:], A.mult))
    v(ts(T.si[:], T.eq[:], c63, None, A.add))
    v(ts(T.se[:], T.eq[:], -1.0, c63, A.mult, A.add))
    vw()

    near_ws = [w for w in range(3) if 0 <= r - 1 + w < n]
    p0, p1 = 16 * near_ws[0], 16 * near_ws[-1] + 16
    s0, s1 = r - 1 + near_ws[0], r + near_ws[-1]
    g.scalar.wait_ge(S.s_ln, 16)
    if edge:
        g.scalar.wait_ge(S.sv, n_edge)
    g.scalar.wait_ge(S.ln_near, len(nb))
    g.scalar.dma_start(T.pl[p0:p1, :], T.lall[s0:s1]).then_inc(S.s_pl, 16)
    g.scalar.dma_start(T.pl[64 + p0:64 + p1, :], T.lall[s0:s1]).then_inc(S.s_pl, 16)
    g.sync.wait_ge(S.s_ln, 16)
    g.sync.wait_ge(S.ln_near, len(nb))
    if far_src:
        g.sync.wait_ge(S.ln_far, far_src)
    g.sync.dma_start(T.la[0:kb, :], T.lall[0:r + 1]).then_inc(S.s_la, 16)

    g.vector.wait_ge(S.s_pl, 32)
    v(g.vector.tensor_copy(T.lf[0:48, 0:64], T.pl[0:48, :]))
    n_lf = v(g.vector.tensor_copy(T.lf[64:112, 64:128], T.pl[64:112, :]))
    vw()
    mul, add = A.mult, A.add
    v(g.vector.tensor_tensor_scan(T.cr[0:48, 0:64], T.ones[0:48, 0:64], T.lf[0:48, 0:64], 0.0, mul, add))
    n_cr = v(g.vector.tensor_tensor_scan(T.cr[0:48, 64:128], T.ones[0:48, 0:64], T.lf[0:48, 0:64], 0.0, mul, add))
    g.vector.wait_ge(S.s_la, 16)
    v(tt(T.s2[0:kb, :], T.la[0:kb, 0:64], T.la[0:kb, 64:128], A.add))
    vw()
    v(g.vector.tensor_reduce(T.tot[0:kb, 0:1], T.s2[0:kb, :], AxisListType.X, A.add))
    vw()
    n_rr = v(ts(T.rr[0:kb, :], T.selt[0:kb, :], T.tot[0:kb, 0:1], T.col[0:kb, 2:3], A.mult, A.add))

    mm = g.tensor.matmul
    ep = T.ep[:, 0:24]
    g.tensor.wait_ge(S.sv, n_lf)
    mm(ep, T.lf[0:112, :], T.selg[0:112, :], True, False)
    g.tensor.wait_ge(S.sv, n_cr)
    mm(ep, T.cr[0:48, :], T.sela[0:48, :], False, False)
    g.tensor.wait_ge(S.sv, n_rr)
    mm(ep, T.ones[0:kb, :], T.rr[0:kb, :], False, True).then_inc(S.sp, 1)

    g.vector.wait_ge(S.sp, 1)
    v(g.vector.tensor_copy(T.ai[:], ep))
    vw()
    n_nf = v(tt(T.nf[:], T.ai[:], ep, A.subtract))
    g.scalar.wait_ge(S.sv, n_nf)
    for c in range(24):
        ts(T.sta[:, 66 * c:66 * c + 65], T.ia[:, 0:65], T.ep[:, c:c + 1], None, A.is_gt).then_inc(S.sa, 1)
        g.scalar.activation(T.stb[:, 64 * c:64 * c + 64], T.beta[:], F.Sign, bias=T.nf[:, c:c + 1]).then_inc(S.sb, 1)
        g.tensor.wait_ge(S.sa, c + 1)
        g.tensor.wait_ge(S.sb, c + 1)
        k = mm(T.yp[0:64, 0:65], T.stb[:, 64 * c:64 * c + 64], T.sta[:, 66 * c:66 * c + 65], c == 0, c == 23)
    k.then_inc(S.sp, 1)

    g.vector.wait_ge(S.sp, 2)
    v(g.vector.tensor_copy(T.xy[0:64, 0:65], T.yp[0:64, 0:65]))
    vw()
    n_xy = v(tt(T.xy[64:128, 0:65], T.yp[0:64, 0:65], T.xy[0:64, 0:65], A.subtract))
    g.tensor.wait_ge(S.sv, n_xy)
    for u in range(4):
        mm(T.cn[:, u:256:4], T.si[:, 128 * u:128 * u + 128], T.xy[:, 1:65], True, False)
        k = mm(T.cn[:, u:256:4], T.se[:, 128 * u:128 * u + 128], T.xy[:, 0:64], False, True)
    k.then_inc(S.sp, 1)
    qs = sum(CH_S)
    g.vector.wait_ge(S.sp, 3)
    n_o1 = v(g.vector.tensor_copy(T.off[:, 0:qs], T.cn[:, 0:qs]))
    n_o2 = v(g.vector.tensor_copy(T.off[:, qs:256], T.cn[:, qs:256]))

    for q in (g.scalar, g.vector):
        q.wait_ge(S.s_x, 16)
        q.wait_ge(S.x_arr, n_off * len(nb))
    g.scalar.wait_ge(S.sv, n_o1)
    vw()
    a, b = 0, qs
    for i in range(max(len(CH_S), len(CH_V))):
        if i < len(CH_S):
            e = a + CH_S[i]
            g.scalar.activation(T.yb[:, 16 * a:16 * e], T.xw[:, 0:3080].indirect(T.off[:, a:e]), F.Copy).then_inc(S.gs, 1)
            g.sync.wait_ge(S.gs, i + 1)
            g.sync.dma_start(T.y[:, 16 * a:16 * e], T.yb[:, 16 * a:16 * e]).then_inc(S.sst, 16)
            a = e
        if i < len(CH_V):
            e = b + CH_V[i]
            g.vector.tensor_copy(T.yb[:, 16 * b:16 * e], T.xw[:, 0:3080].indirect(T.off[:, b:e])).then_inc(S.gv, 1)
            g.sync.wait_ge(S.gv, i + 1)
            g.sync.dma_start(T.y[:, 16 * b:16 * e], T.yb[:, 16 * b:16 * e]).then_inc(S.sst, 16)
            b = e
    g.sync.wait_ge(S.sst, 16 * (len(CH_S) + len(CH_V)))
    g.wait_ge(S.snd_ln, len(tr))
    g.wait_ge(S.snd_x, len(_bits(hm)))
